import numpy as np
import ml_dtypes


def mxq(x, axis, fmt="e4m3"):
    dtype, down = {"e4m3": (ml_dtypes.float8_e4m3fn, 7), "e5m2": (ml_dtypes.float8_e5m2, 14)}[fmt]
    v = np.moveaxis(np.asarray(x, np.float32).astype(ml_dtypes.bfloat16).astype(np.float64), axis, -1)
    blocks = v.reshape(v.shape[:-1] + (-1, 32))
    amax = np.abs(blocks).max(-1, keepdims=True)
    byte = np.maximum(np.where(amax > 0, np.frexp(amax)[1] - 1 + 127, 0) - down, 1)
    scale = np.exp2(byte - 127.0)
    codes = (blocks / scale).astype(np.float32).astype(dtype).astype(np.float64)
    return np.moveaxis((codes * scale).reshape(v.shape), -1, axis)


WIDE = False


def mx_kscale(k):
    if not WIDE:
        return np.ones(k)
    levels = np.array([10, -10, 5, -5, 0])
    if k % 512:
        return np.exp2(np.random.permutation(np.resize(levels, k // 32))).repeat(32)
    a = np.empty((k // 512, 16))
    for p in range(k // 512):
        a[p, :8] = np.random.permutation(np.resize(levels, 8))
        for g in range(8):
            far = levels[np.abs(levels - a[p, g]) >= 10]
            a[p, g + 8] = far[np.random.randint(len(far))]
    return np.exp2(a.ravel()).repeat(32)


def f64(x):
    return np.asarray(x).astype(np.float64)


def striped8(idx):
    return np.asarray(idx).reshape(8, -1, 16).transpose(0, 2, 1).reshape(128, -1).astype(np.uint16)


def unstriped8(offs):
    return offs.reshape(8, 16, -1).transpose(0, 2, 1).reshape(8, -1).astype(np.int64)


def pick8(x, idx, run):
    r = np.arange(len(x))
    return x[r[:, None], idx[r % (8 * run) // run]]


E2M1 = np.array([0.0, 0.5, 1.0, 1.5, 2.0, 3.0, 4.0, 6.0, -0.0, -0.5, -1.0, -1.5, -2.0, -3.0, -4.0, -6.0])


def pack_weight(w, fmt):
    k, n = w.shape
    w = f64(np.asarray(w, np.float32).astype(ml_dtypes.bfloat16)).reshape(k // 32, 32, n)
    amax = np.abs(w).max(1)
    if fmt == "e4m3":
        byte = np.frexp(amax)[1] - 1 + 127 - 7
    else:
        mant, ex = np.frexp(amax / 6.0)
        byte = np.where(mant > 0.5, ex, ex - 1) + 127
    byte = np.clip(np.where(amax > 0, byte, 1), 1, 254)
    scaled = (w * np.exp2(127.0 - byte)[:, None, :]).reshape(k, n).astype(np.float32)
    by_word = np.ascontiguousarray(scaled.reshape(k // 512, 128, 4, n).transpose(0, 1, 3, 2))
    if fmt == "e4m3":
        words = by_word.astype(ml_dtypes.float8_e4m3fn).view(np.uint8)
    else:
        c = by_word.astype(ml_dtypes.float4_e2m1fn).view(np.uint8) & 0xF
        words = (c[..., 0::2] | (c[..., 1::2] << 4)).reshape(k // 512, 128, 2 * n)
    return np.ascontiguousarray(words), np.ascontiguousarray(byte.astype(np.uint8).reshape(k // 512, 16, n))


def unpack_weight(words, scales, fmt):
    g, _, n = scales.shape
    words = np.ascontiguousarray(words).reshape(g, 128, n, -1)
    if fmt == "e4m3":
        vals = words.view(ml_dtypes.float8_e4m3fn).astype(np.float64)
    else:
        nib = np.empty((g, 128, n, 4), np.uint8)
        nib[..., 0::2] = words & 0xF
        nib[..., 1::2] = words >> 4
        vals = E2M1[nib]
    vals = vals * np.repeat(np.exp2(scales.astype(np.float64) - 127.0), 8, axis=1)[..., None]
    return vals.transpose(0, 1, 3, 2).reshape(g * 512, n)


D, T, U, X, I, Q = 512, 1024, 1024, 1024, 512, 128


def setup_inputs():
    n = np.random.standard_normal
    idx = np.stack([np.random.permutation(T)[:I] for _ in range(8)])
    idx2 = np.stack([np.random.permutation(U)[:I] for _ in range(8)])
    idx3 = np.stack([np.random.permutation(X)[:I] for _ in range(8)])
    idx4 = np.stack([np.random.permutation(T)[:I] for _ in range(8)])
    idx5 = np.stack([np.random.permutation(U)[:I] for _ in range(8)])
    idx6 = np.stack([np.random.permutation(X)[:I] for _ in range(8)])
    fd = mx_kscale(D)
    keysp = pack_weight(n((D, T)) / fd[:, None], "e2m1")
    notesp = pack_weight(n((D, U)) / fd[:, None], "e4m3")
    usersp = pack_weight(n((D, X)) / fd[:, None], "e2m1")
    return {
        "query": (n((D, Q)) * 1.0 / np.sqrt(D) * fd[:, None]).astype(np.float32),
        "keys_words": keysp[0],
        "keys_scales": keysp[1],
        "notes_words": notesp[0],
        "notes_scales": notesp[1],
        "users_words": usersp[0],
        "users_scales": usersp[1],
        "offs": striped8(idx),
        "offs2": striped8(idx2),
        "offs3": striped8(idx3),
        "offs4": striped8(idx4),
        "offs5": striped8(idx5),
        "offs6": striped8(idx6),
    }


def reference(query, keys_words, keys_scales, notes_words, notes_scales, users_words, users_scales, offs, offs2, offs3, offs4, offs5, offs6):
    idx = unstriped8(offs)
    idx2 = unstriped8(offs2)
    idx3 = unstriped8(offs3)
    idx4 = unstriped8(offs4)
    idx5 = unstriped8(offs5)
    idx6 = unstriped8(offs6)
    keysu = unpack_weight(keys_words, keys_scales, "e2m1")
    notesu = unpack_weight(notes_words, notes_scales, "e4m3")
    usersu = unpack_weight(users_words, users_scales, "e2m1")
    queryq = mxq(f64(query), 0, "e4m3")
    a = queryq.T @ keysu
    b = queryq.T @ notesu
    c0 = queryq.T @ usersu
    f1 = np.zeros((Q, U))
    f1[np.arange(Q)[:, None], idx2[np.arange(Q) % 128 // 16]] = pick8(a, idx, 16)
    f2 = np.zeros((Q, X))
    f2[np.arange(Q)[:, None], idx3[np.arange(Q) % 128 // 16]] = pick8(b, idx2, 16)
    f3 = np.zeros((Q, T))
    f3[np.arange(Q)[:, None], idx[np.arange(Q) % 128 // 16]] = pick8(c0, idx3, 16)
    aa = a + f3
    bb = b + f1
    cc = c0 - f2
    v = np.maximum(pick8(aa, idx4, 16), pick8(bb, idx5, 16))
    y = v - pick8(cc, idx6, 16)
    return y

from contextlib import ExitStack

import concourse.mybir as mybir

D, COLS, SLOTS, Q = 512, 1024, 512, 128
FLOPS = 2 * D * Q * 3 * COLS

F32 = mybir.dt.float32
BF16 = mybir.dt.bfloat16
I32 = mybir.dt.int32
U32 = mybir.dt.uint32
U16 = mybir.dt.uint16
U8 = mybir.dt.uint8
FP8X4 = mybir.dt.float8_e4m3fn_x4
FP4X4 = mybir.dt.float4_e2m1fn_x4
ALU = mybir.AluOpType
COPY = mybir.ActivationFunctionType.Copy

P = 128
PACK = 4
BANK = 512
HALF = SLOTS // 2
LIST_COLS = SLOTS // 16


def tile_attend_rotation_three_kernel(
    tc, query, keys_words, keys_scales, notes_words, notes_scales, users_words, users_scales,
    offs, offs2, offs3, offs4, offs5, offs6, out,
):
    nc = tc.nc
    with ExitStack() as ctx:
        sb = ctx.enter_context(tc.tile_pool(name="sb", bufs=1))
        ps = ctx.enter_context(tc.psum_pool(name="ps", bufs=1))

        def load_list(name, src):
            t = sb.tile([P, LIST_COLS], U16, name=name)
            nc.sync.dma_start(t[:], src)
            return t

        def load_words(name, src2d):
            t = sb.tile([P, src2d.shape[1]], U8, name=name, tag=name, align_bytes=64)
            nc.sync.dma_start(t[:].bitcast(I32), src2d.bitcast(I32))
            return t

        def clear_plane(name):
            t = sb.tile([P, COLS], U8, name=name, align_bytes=64)
            nc.vector.memset(t[:].bitcast(I32), 0)
            return t

        def load_plane(t, scales):
            for quad in range(4):
                nc.sync.dma_start(
                    t[32 * quad : 32 * quad + 4, :].bitcast(I32),
                    scales[0, 4 * quad : 4 * quad + 4, :].bitcast(I32),
                )

        def cleared(name):
            t = sb.tile([P, COLS], F32, name=name)
            nc.vector.memset(t[:].bitcast(I32), 0)
            return t

        users_plane = clear_plane("users_plane")
        keys_plane = clear_plane("keys_plane")
        notes_plane = clear_plane("notes_plane")
        f3 = cleared("f3")
        f1 = cleared("f1")

        q_raw = sb.tile([P, PACK, Q], F32, name="q_raw")
        nc.sync.dma_start(q_raw[:], query.rearrange("(p j) q -> p j q", j=PACK))
        users_w = load_words("users_w", users_words[0])
        load_plane(users_plane, users_scales)
        l3 = load_list("l3", offs3)
        l1 = load_list("l1", offs)
        keys_w = load_words("keys_w", keys_words[0])
        load_plane(keys_plane, keys_scales)
        l2 = load_list("l2", offs2)
        notes_w = load_words("notes_w", notes_words[0].rearrange("p n t -> p (n t)"))
        load_plane(notes_plane, notes_scales)
        l4 = load_list("l4", offs4)
        l5 = load_list("l5", offs5)
        l6 = load_list("l6", offs6)

        q_bf = sb.tile([P, Q, PACK], BF16, name="q_bf", align_bytes=64)
        nc.vector.tensor_copy(
            q_bf[:, : Q // 2, :].rearrange("p (c i) t -> p c t i", i=4),
            q_raw[:, :, : Q // 2].rearrange("p t (c i) -> p c t i", i=4),
        )
        nc.scalar.copy(
            q_bf[:, Q // 2 :, :].rearrange("p (c i) t -> p c t i", i=4),
            q_raw[:, :, Q // 2 :].rearrange("p t (c i) -> p c t i", i=4),
        )
        q_codes = sb.tile([P, Q], U32, name="q_codes", align_bytes=64)
        q_plane = sb.tile([P, Q], U8, name="q_plane", align_bytes=64)
        nc.vector.quantize_mx(
            out=q_codes[:].bitcast(FP8X4), scales=q_plane[:], in_=q_bf[:].rearrange("p q t -> p (q t)")
        )

        f2 = cleared("f2")

        def scores(name, words, plane, fmt, word_bytes, width):
            banks = []
            for n in range(COLS // width):
                bank = ps.tile([P, width], F32, name=f"{name}_bank{n}")
                nc.tensor.matmul_mx(
                    out=bank[:],
                    lhsT=q_codes[:].bitcast(FP8X4),
                    lhsT_scale=q_plane[:],
                    rhs=words[:, word_bytes * width * n : word_bytes * width * (n + 1)].bitcast(fmt),
                    rhs_scale=plane[:, width * n : width * (n + 1)],
                    start=True,
                    stop=True,
                )
                banks.append(bank)
            return banks

        def half(lst, h):
            return lst[:, h * LIST_COLS // 2 : (h + 1) * LIST_COLS // 2]

        QUARTER = COLS // 4
        c_banks = scores("c0", users_w, users_plane, FP4X4, 2, QUARTER)
        c0 = sb.tile([P, COLS], F32, name="c0")
        for n in range(4):
            dst = c0[:, QUARTER * n : QUARTER * (n + 1)]
            if n % 2 == 0:
                nc.scalar.copy(dst, c_banks[n][:])
            else:
                nc.vector.tensor_copy(dst, c_banks[n][:])
        c_picked = sb.tile([P, SLOTS], F32, name="c_picked")
        nc.vector.tensor_copy(c_picked[:, :HALF], c0[:].indirect(half(l3, 0)))
        nc.scalar.activation(c_picked[:, HALF:], c0[:].indirect(half(l3, 1)), COPY)
        nc.vector.tensor_copy(f3[:].indirect(l1[:]), c_picked[:])

        a_banks = scores("a", keys_w, keys_plane, FP4X4, 2, BANK)
        a = sb.tile([P, COLS], F32, name="a")
        for n in range(2):
            nc.scalar.copy(a[:, BANK * n : BANK * (n + 1)], a_banks[n][:])
        a_picked = sb.tile([P, SLOTS], F32, name="a_picked")
        nc.scalar.activation(a_picked[:], a[:].indirect(l1[:]), COPY)
        nc.vector.tensor_copy(f1[:].indirect(l2[:]), a_picked[:])

        b_banks = scores("b", notes_w, notes_plane, FP8X4, 4, BANK)
        b = sb.tile([P, COLS], F32, name="b")
        for n in range(2):
            nc.scalar.copy(b[:, BANK * n : BANK * (n + 1)], b_banks[n][:])
        b_picked = sb.tile([P, SLOTS], F32, name="b_picked")
        nc.scalar.activation(b_picked[:], b[:].indirect(l2[:]), COPY)
        nc.vector.tensor_copy(f2[:].indirect(l3[:]), b_picked[:])

        aa = sb.tile([P, COLS], F32, name="aa", tag="notes_w", align_bytes=64)
        nc.gpsimd.tensor_tensor(aa[:], a[:], f3[:], ALU.add)
        aa_picked = sb.tile([P, SLOTS], F32, name="aa_picked")
        nc.scalar.activation(aa_picked[:], aa[:].indirect(l4[:]), COPY)
        bb = sb.tile([P, COLS], F32, name="bb")
        nc.gpsimd.tensor_tensor(bb[:], b[:], f1[:], ALU.add)
        bb_picked = sb.tile([P, SLOTS], F32, name="bb_picked")
        nc.scalar.activation(bb_picked[:], bb[:].indirect(l5[:]), COPY)

        cc = sb.tile([P, COLS], F32, name="cc")
        for n in range(3):
            cols = slice(QUARTER * n, QUARTER * (n + 1))
            nc.vector.tensor_tensor(cc[:, cols], c_banks[n][:], f2[:, cols], ALU.subtract)
        cols = slice(QUARTER * 3, COLS)
        nc.gpsimd.tensor_tensor(cc[:, cols], c0[:, cols], f2[:, cols], ALU.subtract)

        v = sb.tile([P, SLOTS], F32, name="v")
        nc.vector.tensor_tensor(v[:], aa_picked[:], bb_picked[:], ALU.max)
        for h in range(2):
            cols = slice(HALF * h, HALF * (h + 1))
            cc_picked = sb.tile([P, HALF], F32, name=f"cc_picked{h}")
            nc.scalar.activation(cc_picked[:], cc[:].indirect(half(l6, h)), COPY)
            y = sb.tile([P, HALF], F32, name=f"y{h}")
            nc.vector.tensor_tensor(y[:], v[:, cols], cc_picked[:], ALU.subtract)
            nc.sync.dma_start(out[:, cols], y[:])
